import numpy as np, ml_dtypes
CORES = [17,57,65,89,97,121]
N = 6
DEG, TK = 3, 512
MASK = [[2,3,0],[2,3,1],[2,3,0],[2,3,0],[2,3,4],[2,3,5]]
def setup_inputs(rng):
    return {"x": rng.standard_normal((N, 128, TK), dtype=np.float32).astype(ml_dtypes.bfloat16), "w": rng.standard_normal((N, 128, DEG * 128), dtype=np.float32).astype(ml_dtypes.bfloat16)}
def setup_inputs_big(rng):
    d = setup_inputs(rng)
    for k in ("x", "w"): d[k] = (d[k].astype(np.float32) * 1024.0).astype(d[k].dtype)
    return d
def setup_inputs_small(rng):
    d = setup_inputs(rng)
    for k in ("x", "w"): d[k] = (d[k].astype(np.float32) * (1 / 1024.0)).astype(d[k].dtype)
    return d
def setup_inputs_apart(rng):
    d = setup_inputs(rng)
    f = (10.0 ** rng.permutation(np.linspace(-1.5, 1.5, N))).astype(np.float32).reshape(N, 1, 1)
    for k in ("x", "w"): d[k] = (d[k].astype(np.float32) * f).astype(d[k].dtype)
    return d
def reference(x, w):
    X, W = x.astype(np.float64), w.astype(np.float64)
    y = np.zeros((N, 128, TK))
    for r in range(N):
        for i, j in enumerate(MASK[r]):
            y[r] += W[r][:, 128 * i:128 * i + 128].T @ X[j]
    return {"y": y.astype(ml_dtypes.bfloat16 if x.dtype != np.float64 else np.float64)}

@@ -1,0 +1,156 @@
+from concourse.bass import DstId, RemoteDMATransfer
+
+NRANKS = 6
+P = 128
+TK = 512
+HALF = TK // 2
+
+SCRATCH = {
+    "wb": ("sbuf", [P, 3 * P], "bfloat16"),
+    "yb": ("sbuf", [P, TK], "bfloat16"),
+    "d0": ("dram", [P, HALF], "bfloat16"),
+    "d1": ("dram", [P, HALF], "bfloat16"),
+    "ps0": ("psum", [P, TK], "float32"),
+    "ps1": ("psum", [P, TK], "float32"),
+}
+for _j in range(NRANKS):
+    SCRATCH["xb%d" % _j] = ("sbuf", [P, TK], "bfloat16")
+
+SEMAPHORES = ["ld0", "ld1", "ldx", "ldw", "sent", "mm0", "mm1", "cp0", "cp1", "st0", "st1"]
+SEMAPHORES += ["s%d_%d" % (_j, _h) for _j in range(NRANKS) for _h in range(2)]
+
+
+def _bits(m):
+    return [e for e in range(m.bit_length()) if (m >> e) & 1]
+
+
+def _mask(engines):
+    m = 0
+    for e in engines:
+        m |= 1 << e
+    return m
+
+
+def _dst(topo, c):
+    a = topo.addr(c)
+    return DstId(rid=a[0], pnc=a[1])
+
+
+def _plan(T, topo):
+    cores = list(T.cores)
+    table = T.tables["MASK"]
+    n = len(cores)
+    every = range(topo.CORES_PER_CHIP * topo.CHIPS)
+    plan = {}
+    for j in range(n):
+        s = cores[j]
+        dests = [cores[r] for r in range(n) if r != j and j in table[r]]
+        if not dests:
+            continue
+        near = [d for d in dests if topo.may_write(s, d)]
+        far = [d for d in dests if not topo.may_write(s, d)]
+        direct = near[:1]
+        relayed = far + near[1:]
+        free = [c for c in every if topo.chip(c) == topo.chip(s) and T.rank_of(c) is None]
+        able = [c for c in free if all(topo.may_write(c, d) for d in relayed)]
+        pools = ([c for c in able if topo.die(c) == topo.die(s)], [c for c in able if topo.die(c) != topo.die(s)])
+        k = min(2, len(relayed))
+        helpers = []
+        if k:
+            away = set(_bits(topo.mask(s, dests[0])))
+            home = [e for e in _bits(topo.mask(s, able[0])) if e not in away]
+            for h in range(2):
+                mine = home[h::2]
+                per = len(mine) // k
+                for i in range(k):
+                    helpers.append((pools[h][i], h, relayed[i::k], mine[i * per:(i + 1) * per]))
+        plan[j] = {"src": s, "direct": direct, "near": near, "helpers": helpers}
+    return plan
+
+
+def rank_program(g, core, T, topo):
+    plan = _plan(T, topo)
+    sem = T.sem
+    cols = (slice(0, HALF), slice(HALF, TK))
+
+    for j in plan:
+        for (hc, h, dl, hop) in plan[j]["helpers"]:
+            if hc != core:
+                continue
+            landed = sem["s%d_%d" % (j, h)]
+            eng = set(_bits(topo.mask(core, dl[0])))
+            for d in dl:
+                eng &= set(_bits(topo.mask(core, d)))
+            eng = sorted(eng)
+            g.wait_ge(landed, len(hop))
+            g.remote_dma_fused(
+                [RemoteDMATransfer(dst_ids=[_dst(topo, d) for d in dl], dma_engine_mask=_mask(eng), remote_sem=landed,
+                                   srcs=[T["d%d" % h][:]], dsts=[T["xb%d" % j][:, cols[h]] for d in dl], alu_op=0)],
+                local_sem=sem.sent)
+            g.wait_ge(sem.sent, len(eng))
+
+    rank = T.rank_of(core)
+    if rank is None:
+        return
+    table = T.tables["MASK"]
+    own = T["xb%d" % rank]
+    mine = plan.get(rank)
+
+    if mine and mine["helpers"]:
+        g.sync.dma_start(T.d0[:], T.x[:, cols[0]]).then_inc(sem.ld0, 16)
+        g.scalar.dma_start(T.d1[:], T.x[:, cols[1]]).then_inc(sem.ld1, 16)
+    g.sync.dma_start(own[:], T.x[:]).then_inc(sem.ldx, 16)
+    g.scalar.dma_start(T.wb[:], T.w[:]).then_inc(sem.ldw, 16)
+
+    sent = 0
+    if mine:
+        if mine["helpers"]:
+            g.wait_ge(sem.ld0, 16)
+            g.wait_ge(sem.ld1, 16)
+            g.remote_dma_fused(
+                [RemoteDMATransfer(dst_ids=[_dst(topo, hc)], dma_engine_mask=_mask(hop),
+                                   remote_sem=sem["s%d_%d" % (rank, h)], src=T["d%d" % h][:], dst=T["d%d" % h][:])
+                 for (hc, h, dl, hop) in mine["helpers"]],
+                local_sem=sem.sent)
+            sent += sum(len(hop) for (hc, h, dl, hop) in mine["helpers"])
+        for d in mine["direct"]:
+            a = topo.addr(d)
+            m = topo.mask(core, d)
+            g.wait_ge(sem.ldx, 16)
+            g.remote_dma(out_ap=own[:], in_ap=own[:], remote_sem=sem["s%d_0" % rank], local_sem=sem.sent,
+                         pid=a[1], routing_id=a[0], dma_engine_mask=m)
+            sent += len(_bits(m))
+
+    work = []
+    for i, j in enumerate(table[rank]):
+        for h in range(2):
+            if j == rank:
+                work.append((0, h, i, j, "ldx", 16))
+            elif core in plan[j]["direct"]:
+                work.append((1, h, i, j, "s%d_0" % j, len(_bits(topo.mask(plan[j]["src"], core)))))
+            else:
+                hc = [x[0] for x in plan[j]["helpers"] if x[1] == h and core in x[2]][0]
+                load = [len(x[2]) for x in plan[j]["helpers"] if x[0] == hc][0]
+                late = 2 if core in plan[j]["near"] else 3
+                work.append((late, load, h, i, j, "s%d_%d" % (j, h), len(_bits(topo.mask(hc, core)))))
+    work.sort()
+    todo = [len(table[rank])] * 2
+    left = list(todo)
+    g.tensor.wait_ge(sem.ldw, 16)
+    for item in work:
+        h, i, j, name, count = item[-5:]
+        g.tensor.wait_ge(sem[name], count)
+        g.tensor.matmul(T["ps%d" % h][:, 0:HALF], T.wb[:, P * i:P * (i + 1)], T["xb%d" % j][:, cols[h]],
+                        left[h] == todo[h], left[h] == 1).then_inc(sem["mm%d" % h], 1)
+        left[h] -= 1
+
+    for h, q in ((0, g.sync), (1, g.scalar)):
+        g.vector.wait_ge(sem["mm%d" % h], todo[h])
+        g.vector.tensor_copy(T.yb[:, cols[h]], T["ps%d" % h][:, 0:HALF]).then_inc(sem["cp%d" % h], 1)
+        q.wait_ge(sem["cp%d" % h], 1)
+        q.dma_start(T.y[:, cols[h]], T.yb[:, cols[h]]).then_inc(sem["st%d" % h], 16)
+
+    if sent:
+        g.wait_ge(sem.sent, sent)
+    g.wait_ge(sem.st0, 16)
+    g.wait_ge(sem.st1, 16)

@@ -3,21 +3,23 @@ from concourse.bass import DstId, RemoteDMATransfer
 NRANKS = 6
 P = 128
 TK = 512
-HALF = TK // 2
+NQ = 4
+QW = TK // NQ
 
 SCRATCH = {
     "wb": ("sbuf", [P, 3 * P], "bfloat16"),
     "yb": ("sbuf", [P, TK], "bfloat16"),
-    "d0": ("dram", [P, HALF], "bfloat16"),
-    "d1": ("dram", [P, HALF], "bfloat16"),
-    "ps0": ("psum", [P, TK], "float32"),
-    "ps1": ("psum", [P, TK], "float32"),
 }
+for _q in range(NQ):
+    SCRATCH["dq%d" % _q] = ("dram", [P, QW], "bfloat16")
+    SCRATCH["ps%d" % _q] = ("psum", [P, TK], "float32")
 for _j in range(NRANKS):
     SCRATCH["xb%d" % _j] = ("sbuf", [P, TK], "bfloat16")
 
-SEMAPHORES = ["ld0", "ld1", "ldx", "ldw", "sent", "mm0", "mm1", "cp0", "cp1", "st0", "st1"]
-SEMAPHORES += ["s%d_%d" % (_j, _h) for _j in range(NRANKS) for _h in range(2)]
+SEMAPHORES = ["ldq", "ldx", "ldw", "hop", "sent", "cp0", "cp1", "st0", "st1"]
+SEMAPHORES += ["mm%d" % _q for _q in range(NQ)]
+SEMAPHORES += ["sd%d" % _j for _j in range(NRANKS)]
+SEMAPHORES += ["s%d_%d" % (_j, _q) for _j in range(NRANKS) for _q in range(NQ)]
 
 
 def _bits(m):
@@ -49,43 +51,44 @@ def _plan(T, topo):
             continue
         near = [d for d in dests if topo.may_write(s, d)]
         far = [d for d in dests if not topo.may_write(s, d)]
-        direct = near[:1]
-        relayed = far + near[1:]
-        free = [c for c in every if topo.chip(c) == topo.chip(s) and T.rank_of(c) is None]
-        able = [c for c in free if all(topo.may_write(c, d) for d in relayed)]
-        pools = ([c for c in able if topo.die(c) == topo.die(s)], [c for c in able if topo.die(c) != topo.die(s)])
-        k = min(2, len(relayed))
         helpers = []
-        if k:
-            away = set(_bits(topo.mask(s, dests[0])))
+        if far:
+            free = [c for c in every if topo.chip(c) == topo.chip(s) and T.rank_of(c) is None]
+            able = [c for c in free if all(topo.may_write(c, d) for d in far)]
+            pools = ([c for c in able if topo.die(c) == topo.die(s)], [c for c in able if topo.die(c) != topo.die(s)])
+            away = set(_bits(topo.mask(s, far[0])))
             home = [e for e in _bits(topo.mask(s, able[0])) if e not in away]
-            for h in range(2):
-                mine = home[h::2]
-                per = len(mine) // k
-                for i in range(k):
-                    helpers.append((pools[h][i], h, relayed[i::k], mine[i * per:(i + 1) * per]))
-        plan[j] = {"src": s, "direct": direct, "near": near, "helpers": helpers}
+            for q in range(NQ):
+                side, i = divmod(q, NQ // 2)
+                lane = home[side::2]
+                per = len(lane) // (NQ // 2)
+                hc = pools[side][i]
+                eng = set(_bits(topo.mask(hc, far[0])))
+                for d in far:
+                    eng &= set(_bits(topo.mask(hc, d)))
+                eng = sorted(eng)
+                if len(far) == 1:
+                    eng = eng[::2]
+                helpers.append((hc, q, lane[i * per:(i + 1) * per], eng))
+        plan[j] = {"src": s, "near": near, "far": far, "helpers": helpers}
     return plan
 
 
 def rank_program(g, core, T, topo):
     plan = _plan(T, topo)
     sem = T.sem
-    cols = (slice(0, HALF), slice(HALF, TK))
+    cols = [slice(QW * q, QW * (q + 1)) for q in range(NQ)]
 
     for j in plan:
-        for (hc, h, dl, hop) in plan[j]["helpers"]:
+        for (hc, q, hop, eng) in plan[j]["helpers"]:
             if hc != core:
                 continue
-            landed = sem["s%d_%d" % (j, h)]
-            eng = set(_bits(topo.mask(core, dl[0])))
-            for d in dl:
-                eng &= set(_bits(topo.mask(core, d)))
-            eng = sorted(eng)
-            g.wait_ge(landed, len(hop))
+            far = plan[j]["far"]
+            g.wait_ge(sem.hop, len(hop))
             g.remote_dma_fused(
-                [RemoteDMATransfer(dst_ids=[_dst(topo, d) for d in dl], dma_engine_mask=_mask(eng), remote_sem=landed,
-                                   srcs=[T["d%d" % h][:]], dsts=[T["xb%d" % j][:, cols[h]] for d in dl], alu_op=0)],
+                [RemoteDMATransfer(dst_ids=[_dst(topo, d) for d in far], dma_engine_mask=_mask(eng),
+                                   remote_sem=sem["s%d_%d" % (j, q)], srcs=[T["dq%d" % q][:]],
+                                   dsts=[T["xb%d" % j][:, cols[q]] for d in far], alu_op=0)],
                 local_sem=sem.sent)
             g.wait_ge(sem.sent, len(eng))
 
@@ -97,58 +100,63 @@ def rank_program(g, core, T, topo):
     mine = plan.get(rank)
 
     if mine and mine["helpers"]:
-        g.sync.dma_start(T.d0[:], T.x[:, cols[0]]).then_inc(sem.ld0, 16)
-        g.scalar.dma_start(T.d1[:], T.x[:, cols[1]]).then_inc(sem.ld1, 16)
+        for q in range(NQ):
+            lq = g.sync if q < NQ // 2 else g.scalar
+            lq.dma_start(T["dq%d" % q][:], T.x[:, cols[q]]).then_inc(sem.ldq, 16)
     g.sync.dma_start(own[:], T.x[:]).then_inc(sem.ldx, 16)
     g.scalar.dma_start(T.wb[:], T.w[:]).then_inc(sem.ldw, 16)
 
     sent = 0
     if mine:
         if mine["helpers"]:
-            g.wait_ge(sem.ld0, 16)
-            g.wait_ge(sem.ld1, 16)
+            g.wait_ge(sem.ldq, 16 * NQ)
             g.remote_dma_fused(
-                [RemoteDMATransfer(dst_ids=[_dst(topo, hc)], dma_engine_mask=_mask(hop),
-                                   remote_sem=sem["s%d_%d" % (rank, h)], src=T["d%d" % h][:], dst=T["d%d" % h][:])
-                 for (hc, h, dl, hop) in mine["helpers"]],
+                [RemoteDMATransfer(dst_ids=[_dst(topo, hc)], dma_engine_mask=_mask(hop), remote_sem=sem.hop,
+                                   src=T["dq%d" % q][:], dst=T["dq%d" % q][:])
+                 for (hc, q, hop, eng) in mine["helpers"]],
                 local_sem=sem.sent)
-            sent += sum(len(hop) for (hc, h, dl, hop) in mine["helpers"])
-        for d in mine["direct"]:
-            a = topo.addr(d)
-            m = topo.mask(core, d)
+            sent += sum(len(hop) for (hc, q, hop, eng) in mine["helpers"])
+        if mine["near"]:
+            near = mine["near"]
+            eng = set(_bits(topo.mask(core, near[0])))
+            for d in near:
+                eng &= set(_bits(topo.mask(core, d)))
             g.wait_ge(sem.ldx, 16)
-            g.remote_dma(out_ap=own[:], in_ap=own[:], remote_sem=sem["s%d_0" % rank], local_sem=sem.sent,
-                         pid=a[1], routing_id=a[0], dma_engine_mask=m)
-            sent += len(_bits(m))
+            g.remote_dma_fused(
+                [RemoteDMATransfer(dst_ids=[_dst(topo, d) for d in near], dma_engine_mask=_mask(sorted(eng)),
+                                   remote_sem=sem["sd%d" % rank], srcs=[own[:]], dsts=[own[:] for d in near],
+                                   alu_op=0)],
+                local_sem=sem.sent)
+            sent += len(eng)
 
     work = []
     for i, j in enumerate(table[rank]):
-        for h in range(2):
+        for q in range(NQ):
             if j == rank:
-                work.append((0, h, i, j, "ldx", 16))
-            elif core in plan[j]["direct"]:
-                work.append((1, h, i, j, "s%d_0" % j, len(_bits(topo.mask(plan[j]["src"], core)))))
+                work.append((0, 0, q, i, j, "ldx", 16))
+            elif core in plan[j]["near"]:
+                work.append((1, len(plan[j]["near"]), q, i, j, "sd%d" % j,
+                             len(_bits(topo.mask(plan[j]["src"], core)))))
             else:
-                hc = [x[0] for x in plan[j]["helpers"] if x[1] == h and core in x[2]][0]
-                load = [len(x[2]) for x in plan[j]["helpers"] if x[0] == hc][0]
-                late = 2 if core in plan[j]["near"] else 3
-                work.append((late, load, h, i, j, "s%d_%d" % (j, h), len(_bits(topo.mask(hc, core)))))
+                work.append((2, len(plan[j]["far"]), q, i, j, "s%d_%d" % (j, q), len(plan[j]["helpers"][q][3])))
     work.sort()
-    todo = [len(table[rank])] * 2
-    left = list(todo)
+    deg = len(table[rank])
+    left = [deg] * NQ
     g.tensor.wait_ge(sem.ldw, 16)
     for item in work:
-        h, i, j, name, count = item[-5:]
+        q, i, j, name, count = item[-5:]
         g.tensor.wait_ge(sem[name], count)
-        g.tensor.matmul(T["ps%d" % h][:, 0:HALF], T.wb[:, P * i:P * (i + 1)], T["xb%d" % j][:, cols[h]],
-                        left[h] == todo[h], left[h] == 1).then_inc(sem["mm%d" % h], 1)
-        left[h] -= 1
+        g.tensor.matmul(T["ps%d" % q][:, 0:QW], T.wb[:, P * i:P * (i + 1)], T["xb%d" % j][:, cols[q]],
+                        left[q] == deg, left[q] == 1).then_inc(sem["mm%d" % q], 1)
+        left[q] -= 1
 
-    for h, q in ((0, g.sync), (1, g.scalar)):
-        g.vector.wait_ge(sem["mm%d" % h], todo[h])
-        g.vector.tensor_copy(T.yb[:, cols[h]], T["ps%d" % h][:, 0:HALF]).then_inc(sem["cp%d" % h], 1)
-        q.wait_ge(sem["cp%d" % h], 1)
-        q.dma_start(T.y[:, cols[h]], T.yb[:, cols[h]]).then_inc(sem["st%d" % h], 16)
+    for q in range(NQ):
+        g.vector.wait_ge(sem["mm%d" % q], deg)
+        g.vector.tensor_copy(T.yb[:, cols[q]], T["ps%d" % q][:, 0:QW]).then_inc(sem["cp%d" % (q // (NQ // 2))], 1)
+    hw = TK // 2
+    for h, sq in ((0, g.sync), (1, g.scalar)):
+        sq.wait_ge(sem["cp%d" % h], NQ // 2)
+        sq.dma_start(T.y[:, hw * h:hw * (h + 1)], T.yb[:, hw * h:hw * (h + 1)]).then_inc(sem["st%d" % h], 16)
 
     if sent:
         g.wait_ge(sem.sent, sent)

from concourse.bass import DstId, RemoteDMATransfer

NRANKS = 6
P = 128
TK = 512
NQ = 4
QW = TK // NQ

SCRATCH = {
    "wb": ("sbuf", [P, 3 * P], "bfloat16"),
    "yb": ("sbuf", [P, TK], "bfloat16"),
}
for _q in range(NQ):
    SCRATCH["dq%d" % _q] = ("dram", [P, QW], "bfloat16")
    SCRATCH["ps%d" % _q] = ("psum", [P, TK], "float32")
for _j in range(NRANKS):
    SCRATCH["xb%d" % _j] = ("sbuf", [P, TK], "bfloat16")

SEMAPHORES = ["ldq", "ldx", "ldw", "hop", "sent", "cp0", "cp1", "st0", "st1"]
SEMAPHORES += ["mm%d" % _q for _q in range(NQ)]
SEMAPHORES += ["sd%d" % _j for _j in range(NRANKS)]
SEMAPHORES += ["s%d_%d" % (_j, _q) for _j in range(NRANKS) for _q in range(NQ)]


def _bits(m):
    return [e for e in range(m.bit_length()) if (m >> e) & 1]


def _mask(engines):
    m = 0
    for e in engines:
        m |= 1 << e
    return m


def _dst(topo, c):
    a = topo.addr(c)
    return DstId(rid=a[0], pnc=a[1])


def _plan(T, topo):
    cores = list(T.cores)
    table = T.tables["MASK"]
    n = len(cores)
    every = range(topo.CORES_PER_CHIP * topo.CHIPS)
    plan = {}
    for j in range(n):
        s = cores[j]
        dests = [cores[r] for r in range(n) if r != j and j in table[r]]
        if not dests:
            continue
        near = [d for d in dests if topo.may_write(s, d)]
        far = [d for d in dests if not topo.may_write(s, d)]
        helpers = []
        if far:
            free = [c for c in every if topo.chip(c) == topo.chip(s) and T.rank_of(c) is None]
            able = [c for c in free if all(topo.may_write(c, d) for d in far)]
            pools = ([c for c in able if topo.die(c) == topo.die(s)], [c for c in able if topo.die(c) != topo.die(s)])
            away = set(_bits(topo.mask(s, far[0])))
            home = [e for e in _bits(topo.mask(s, able[0])) if e not in away]
            for q in range(NQ):
                side, i = divmod(q, NQ // 2)
                lane = home[side::2]
                per = len(lane) // (NQ // 2)
                hc = pools[side][i]
                eng = set(_bits(topo.mask(hc, far[0])))
                for d in far:
                    eng &= set(_bits(topo.mask(hc, d)))
                eng = sorted(eng)
                if len(far) == 1:
                    eng = eng[::2]
                helpers.append((hc, q, lane[i * per:(i + 1) * per], eng))
        plan[j] = {"src": s, "near": near, "far": far, "helpers": helpers}
    return plan


def rank_program(g, core, T, topo):
    plan = _plan(T, topo)
    sem = T.sem
    cols = [slice(QW * q, QW * (q + 1)) for q in range(NQ)]

    for j in plan:
        for (hc, q, hop, eng) in plan[j]["helpers"]:
            if hc != core:
                continue
            far = plan[j]["far"]
            g.wait_ge(sem.hop, len(hop))
            g.remote_dma_fused(
                [RemoteDMATransfer(dst_ids=[_dst(topo, d) for d in far], dma_engine_mask=_mask(eng),
                                   remote_sem=sem["s%d_%d" % (j, q)], srcs=[T["dq%d" % q][:]],
                                   dsts=[T["xb%d" % j][:, cols[q]] for d in far], alu_op=0)],
                local_sem=sem.sent)
            g.wait_ge(sem.sent, len(eng))

    rank = T.rank_of(core)
    if rank is None:
        return
    table = T.tables["MASK"]
    own = T["xb%d" % rank]
    mine = plan.get(rank)

    if mine and mine["helpers"]:
        for q in range(NQ):
            lq = g.sync if q < NQ // 2 else g.scalar
            lq.dma_start(T["dq%d" % q][:], T.x[:, cols[q]]).then_inc(sem.ldq, 16)
    g.sync.dma_start(own[:], T.x[:]).then_inc(sem.ldx, 16)
    g.scalar.dma_start(T.wb[:], T.w[:]).then_inc(sem.ldw, 16)

    sent = 0
    if mine:
        if mine["helpers"]:
            g.wait_ge(sem.ldq, 16 * NQ)
            g.remote_dma_fused(
                [RemoteDMATransfer(dst_ids=[_dst(topo, hc)], dma_engine_mask=_mask(hop), remote_sem=sem.hop,
                                   src=T["dq%d" % q][:], dst=T["dq%d" % q][:])
                 for (hc, q, hop, eng) in mine["helpers"]],
                local_sem=sem.sent)
            sent += sum(len(hop) for (hc, q, hop, eng) in mine["helpers"])
        if mine["near"]:
            near = mine["near"]
            eng = set(_bits(topo.mask(core, near[0])))
            for d in near:
                eng &= set(_bits(topo.mask(core, d)))
            g.wait_ge(sem.ldx, 16)
            g.remote_dma_fused(
                [RemoteDMATransfer(dst_ids=[_dst(topo, d) for d in near], dma_engine_mask=_mask(sorted(eng)),
                                   remote_sem=sem["sd%d" % rank], srcs=[own[:]], dsts=[own[:] for d in near],
                                   alu_op=0)],
                local_sem=sem.sent)
            sent += len(eng)

    work = []
    for i, j in enumerate(table[rank]):
        for q in range(NQ):
            if j == rank:
                work.append((0, 0, q, i, j, "ldx", 16))
            elif core in plan[j]["near"]:
                work.append((1, len(plan[j]["near"]), q, i, j, "sd%d" % j,
                             len(_bits(topo.mask(plan[j]["src"], core)))))
            else:
                work.append((2, len(plan[j]["far"]), q, i, j, "s%d_%d" % (j, q), len(plan[j]["helpers"][q][3])))
    work.sort()
    deg = len(table[rank])
    left = [deg] * NQ
    g.tensor.wait_ge(sem.ldw, 16)
    for item in work:
        q, i, j, name, count = item[-5:]
        g.tensor.wait_ge(sem[name], count)
        g.tensor.matmul(T["ps%d" % q][:, 0:QW], T.wb[:, P * i:P * (i + 1)], T["xb%d" % j][:, cols[q]],
                        left[q] == deg, left[q] == 1).then_inc(sem["mm%d" % q], 1)
        left[q] -= 1

    for q in range(NQ):
        g.vector.wait_ge(sem["mm%d" % q], deg)
        g.vector.tensor_copy(T.yb[:, cols[q]], T["ps%d" % q][:, 0:QW]).then_inc(sem["cp%d" % (q // (NQ // 2))], 1)
    hw = TK // 2
    for h, sq in ((0, g.sync), (1, g.scalar)):
        sq.wait_ge(sem["cp%d" % h], NQ // 2)
        sq.dma_start(T.y[:, hw * h:hw * (h + 1)], T.yb[:, hw * h:hw * (h + 1)]).then_inc(sem["st%d" % h], 16)

    if sent:
        g.wait_ge(sem.sent, sent)
    g.wait_ge(sem.st0, 16)
    g.wait_ge(sem.st1, 16)
